import numpy as np, ml_dtypes
CORES = [16,17,18,19,32,33,34,35]
N = 8
BF = ml_dtypes.bfloat16
def gentries(a):
    return np.ascontiguousarray(a.reshape(8, 16, -1).transpose(0, 2, 1)).reshape(8, -1)
def gtable(e):
    e = np.asarray(e); return np.ascontiguousarray(e.reshape(8, -1, 16).transpose(0, 2, 1)).reshape(128, -1).astype(np.int32)
L, T, B, RO = 3072, 3, 512, 2
W = L + T * B
def forest(rng, way):
    k = np.zeros((N, 8, RO, T, 2 * B), np.int64)
    for q in range(N):
        for g in range(8):
            for r in range(RO):
                free = np.ones(W, bool); m = int(way[q, g, r])
                for t in range(T):
                    pool = np.flatnonzero(free[:L + t * B])
                    if m == 0: p = rng.permutation(pool)[:2 * B]
                    elif m == 1: p = pool[:2 * B]
                    else: p = pool[len(pool) - 2 * B:]
                    if m > 0 and rng.random() < 0.5: p = rng.permutation(p)
                    free[p] = False; k[q, g, r, t] = p
    return k
def planned(rng, m, s):
    free = np.ones(W, bool); k = np.zeros((T, 2 * B), np.int64); order = rng.permutation(16); seq = None
    for t in range(T):
        pool = rng.permutation(np.flatnonzero(free[:L + t * B])); node = pool >= L; p = pool[:2 * B]
        if m == 0:
            late = node if t < 2 and t < T - 1 else ~node
            p = rng.permutation(pool[np.argsort(late, kind="stable")][:2 * B])
        elif m == 1 and t == 1:
            p = np.concatenate([pool[node], pool[~node][:B]])
        elif m == 2 and t == 1:
            p = np.concatenate([pool[~node][:B], pool[node]])
        elif m == 3:
            if t == 0:
                near = 128 * int(rng.integers(0, L // 128)) + rng.permutation(128); at = np.arange(2 * B)
                put = rng.permutation(np.flatnonzero(at % N == int(rng.integers(0, N))))[:128]
                rest = np.ones(2 * B, bool); rest[put] = False
                seq = np.zeros(2 * B, np.int64); seq[put] = near; seq[rest] = pool[~np.isin(pool, near)][:2 * B - 128]
            n = len(seq) // 2; slot = np.arange(n) if t == T - 1 else rng.permutation(B)[:n]
            p = np.zeros(2 * B, np.int64); rest = np.ones(2 * B, bool)
            rest[slot] = False; rest[B + slot] = False; p[slot] = seq[0::2]; p[B + slot] = seq[1::2]
            p[rest] = pool[~np.isin(pool, seq)][:2 * B - 2 * n]; seq = L + t * B + slot
        elif m == 4:
            two = np.isin(pool % 16, order[:2]); late = two if t < T - 1 else ~two
            p = rng.permutation(pool[np.argsort(late, kind="stable")][:2 * B])
        elif m == 5 and t == 0:
            p = rng.permutation(pool[np.argsort(order[pool % 16], kind="stable")][:2 * B])
        elif m == 6 and t == 0 and s is not None:
            p = p[np.argsort(s[p], kind="stable")]; i = rng.permutation(B); p = np.concatenate([p[:B][i], p[B:][i]])
        free[p] = False; k[t] = p
    return k
def parts(rng, way=None):
    x = rng.integers(-128, 128, (N, 8, 16, L)); k = forest(rng, np.zeros((N, 8, RO)) if way is None else way)
    a = rng.integers(-1, 2, (N, 8, 16, 16)); b = rng.integers(-1, 2, (N, 8, 16, 16)); w = rng.integers(-127, 128, (N, 8, 16))
    return x, k, a, b, w
def blocks(m):
    o = np.zeros((N, 8, 16, 8, 16), np.float32)
    for g in range(8): o[:, g, :, g, :] = m[:, g]
    return o.reshape(N, 128, 128).astype(BF)
def pack(x, k, a, b, w):
    return {"x": np.ascontiguousarray(x.reshape(N, 128, L)).astype(np.float32).astype(BF), "kids": np.stack([gtable(e.reshape(8, -1)) for e in k]),
            "ml": blocks(a), "mr": blocks(b), "w": w.reshape(N, 128, 1).astype(np.float32).astype(BF)}
def setup_inputs(rng):
    return pack(*parts(rng))
def setup_inputs_runs(rng):
    way = rng.choice(np.array([0, 1, 1, 2, 2]), (N, 8, RO)); i = rng.permutation(8); way[:, i[0]] = 1; way[:, i[1]] = 2
    return pack(*parts(rng, way))
def setup_inputs_ends(rng):
    x, k, a, b, w = parts(rng)
    x = rng.choice(np.array([-128, -127, -1, 0, 1, 126, 127]), (N, 8, 16, L))
    x[:, 0] = rng.integers(126, 128, (N, 16, L)); x[:, 1] = rng.integers(-128, -126, (N, 16, L)); a[:, :2] = 1; b[:, :2] = 1
    x[:, 2] = rng.choice(np.array([-128, 127]), (N, 1, L)); x[:, 2, 0] = rng.integers(-128, 128, (N, L)); a[:, 2] = 1; b[:, 2] = -1
    x[:, 3] = rng.integers(-2, 3, (N, 16, L))
    return pack(x, k, a, b, rng.choice(np.array([-127, 127]), (N, 8, 16)))
def setup_inputs_ties(rng):
    x, k, a, b, w = parts(rng)
    w[:, 0::4] = 0
    w[:, 1::4] = 0; w[:, 1::4, 0] = rng.integers(1, 128, (N, 2)); x[:, 1::4, 0] = rng.integers(-4, 5, (N, 2, L))
    for m in (a, b):
        m[:, 1::4, :, 0] = 0; m[:, 1::4, 0, 0] = 1
    v = rng.integers(-128, 128, (N, 2, 16, 1)); o = np.argsort(rng.random((N, 2, 16, L)), axis=2)
    x[:, 2::4] = np.take_along_axis(np.ascontiguousarray(np.broadcast_to(v, (N, 2, 16, L))), o, 2); w[:, 2::4] = rng.integers(1, 128, (N, 2, 1))
    x[:, 3::4, 2:] = 127; x[:, 3::4, 1] = rng.integers(-1, 2, (N, 2, L)); w[:, 3::4] = 127; w[:, 3::4, 0] = 0; w[:, 3::4, 1] = 1
    return pack(x, k, a, b, w)
def setup_inputs_crowd(rng):
    x, k, a, b, w = parts(rng); o = [int(g) for g in rng.permutation(8)]
    for i, v, c in ((2, 127, -1), (7, -127, 1)):
        x[:, o[i]] = np.where(rng.random((N, 1, L)) < 0.25, -128, rng.integers(-128, -99, (N, 16, L))); w[:, o[i]] = v; a[:, o[i]] = c; b[:, o[i]] = c
    w[:, o[3]] = 0
    for q in range(N):
        for i in range(8):
            s = np.add.reduce(w[q, o[i]][:, None] * x[q, o[i]], axis=0)
            for r in range(RO): k[q, o[i], r] = planned(rng, i if i < 7 else 1, s if r == 0 else None)
    return pack(x, k, a, b, w)
def setup_inputs_spread(rng):
    x, k, a, b, w = parts(rng)
    x = np.rint(127 * rng.uniform(-1, 1, (N, 8, 16, L)) * np.exp2(-rng.integers(0, 7, (N, 8, 1, L)).astype(np.float64))).astype(np.int64) * (rng.random((N, 8, 1, L)) > 0.0625)
    w = np.rint(127 * rng.uniform(-1, 1, (N, 8, 16)) * np.exp2(-rng.integers(0, 7, (N, 8, 16)).astype(np.float64))).astype(np.int64)
    s = rng.uniform(0.2, 1, (N, 8, 1, 1)); a = a * (rng.random(a.shape) < s); b = b * (rng.random(b.shape) < s)
    return pack(x, k, a, b, w)
def check_inputs(d):
    bad = []; own = np.kron(np.eye(8), np.ones((16, 16))) > 0
    for n, lo, hi in (("x", -128, 127), ("ml", -1, 1), ("mr", -1, 1), ("w", -127, 127)):
        v = np.asarray(d[n]).astype(np.float32)
        if not np.all((v == np.floor(v)) & (v >= lo) & (v <= hi)): bad.append("whole numbers of " + n)
        if n in ("ml", "mr") and not np.all(v[:, ~own] == 0): bad.append("zeros of " + n)
    k = np.stack([gentries(e) for e in d["kids"]]).astype(np.int64).reshape(N, 8, RO, T, 2 * B)
    for t in range(T):
        if np.min(k[:, :, :, t]) < 0 or np.max(k[:, :, :, t]) >= L + t * B: bad.append("range of kids")
    if not np.all(np.diff(np.sort(k.reshape(N, 8, RO, -1), axis=3), axis=3) > 0): bad.append("kids used twice")
    return bad
def reference(x, kids, ml, mr, w):
    leaf = x.astype(np.float64).reshape(N, 8, 16, L); ws = w.astype(np.float64).reshape(N, 8, 16, 1)
    cl, cr = [np.stack([m.astype(np.float64)[:, 16 * g:16 * g + 16, 16 * g:16 * g + 16] for g in range(8)], axis=1).transpose(0, 1, 3, 2) for m in (ml, mr)]
    kk = np.stack([gentries(e) for e in kids]).astype(np.int64).reshape(N, 8, RO, T, 2, B)
    for r in range(RO):
        h = np.zeros((N, 8, 16, W)); h[..., :L] = leaf
        size = np.ones((N, 8, W), np.int64); root = np.ones((N, 8, W), bool); order = []
        for t in range(T):
            a, b = kk[:, :, r, t, 0], kk[:, :, r, t, 1]; lo = L + t * B
            ha = np.take_along_axis(h, a[:, :, None, :], 3); hb = np.take_along_axis(h, b[:, :, None, :], 3)
            h[..., lo:lo + B] = np.clip(np.floor((np.matmul(cl, ha) + np.matmul(cr, hb)) * 0.25), -127, 127)
            size[..., lo:lo + B] = np.take_along_axis(size, a, 2) + np.take_along_axis(size, b, 2)
            swap = np.add.reduce(ws * ha, axis=2) < np.add.reduce(ws * hb, axis=2)
            np.put_along_axis(root, a, False, 2); np.put_along_axis(root, b, False, 2)
            order.append((np.where(swap, b, a), np.where(swap, a, b)))
        rs = np.where(root, size, 0); start = np.add.accumulate(rs, axis=2) - rs
        for t in range(T - 1, -1, -1):
            one, two = order[t]; s = start[..., L + t * B:L + t * B + B].copy()
            np.put_along_axis(start, one, s, 2); np.put_along_axis(start, two, s + np.take_along_axis(size, one, 2), 2)
        at = np.argsort(start[..., :L], axis=2)
        new = np.take_along_axis(leaf, at[:, :, None, :], 3).reshape(N, 8, 16, L // N, N)
        leaf = np.ascontiguousarray(new.transpose(4, 1, 2, 0, 3)).reshape(N, 8, 16, L)
    return {"y": leaf.reshape(N, 128, L).astype(np.float32).astype(BF)}

from concourse.bass import DstId, RemoteDMATransfer
from concourse.mybir import AluOpType as OP, ActivationFunctionType as AF, AxisListType as AX

L, NB, RO = 3072, 512, 2
MAGIC = 12582912.0
MAG128 = MAGIC * 128.0
EPOCH = (64.0, 4096.0)
OFFS = 1536.0

SIZE = {"f": 4, "b": 2, "h": 2, "u": 2, "i": 4}
TOP = {k: 0 for k in SIZE}
LAY = {}


def _al(pool, names, tag=""):
    a = 32 // SIZE[pool]
    for item in names.split():
        name, n = item.split(":")
        LAY[name + tag] = (pool, TOP[pool], int(n))
        TOP[pool] += (int(n) + a - 1) // a * a


_al("f", "WA:4096 WD:4096 VA:3104 VD:3104 V0:512 V1:512 V2:512 TR:1032 TB2:1032 IO0:1024 IO1:2048 IOP:1024 ZT:256 PM8:1 BIGC:1 "
         "PLa:64 PL:64 FXA:24 FXD:24 TAa:192 TAb:192 TDa:192 TDb:192")
_al("b", "H0:4096 H1:4096 H2:3072 F:2304 ONES:512 CR:128 TRS:128 Y1:144 T9:9 WS:144 ML:128 MR:128 ML4:128 MR4:128 W:1 BH:128 BON:128 "
         "TRI:128 EYE:128 HA0:1024 HA1:1024 HA2:1024 NT:512 TS:520 GS:1024 CA:1024 CB:1024 CC:1024")
_al("i", "K:384 PI:1 PM:1")
_al("h", "G1:512 G2:1024")
for _r in "01":
    _al("f", "Kf:192 t1:192 t2:192 IA:256 ID:256 JA:256 JD:256 red:1 EN:97 comb:256 miss:64 SZ:192 sz1:32 EX:193 T:200 RS:96 sv:64 "
             "big:64 svb:64 ADD:32 n1:128 n2:128 IDS:192 SUM:160 TB:24 nb:1 af:64 colf:64 cp:96 SW:192 P:192 szf:96 Q:192 i0:32 m:32 "
             "y:96 p1:96 p2:96", _r)
    _al("b", "XP:3072 STG:2304 RSb:288 s1b:32 rb:1 inv:64 bs:64", _r)
    _al("h", "I2:96 X1:64 X2:64 A:96 B:96 inh:192 PRE:64", _r)
    _al("u", "KU:192 SU:192 LS:64 L1:32 L2:64 a16:64 c16:64 OFF:96 AT:192 LP:96", _r)
    _al("i", "kc:192", _r)

DT = {"f": "float32", "b": "bfloat16", "h": "float16", "u": "uint16", "i": "int32"}
SCRATCH = {"pool" + k: ("sbuf", [128, TOP[k]], DT[k]) for k in SIZE}
SCRATCH["roots"] = ("sbuf", [128, 8 * RO, 24], "float32")
for _k in range(8):
    SCRATCH["ps%d" % _k] = ("psum", [128, 512], "float32")
NDMA = 40
NCH = 2
SEMAPHORES = (["cv", "ca", "ct", "cg", "sent"] + ["d%d" % i for i in range(NDMA)]
              + [n + r for r in "01" for n in ("xp", "lp", "own", "far")] + ["h%d" % i for i in range(RO * NCH)])
MARKS = ("aaaaaaaavvvv", "aaaaaaaaaaaa")
DIGITS = "0123456789abcdefghijklmnopqrstuv"
ORDER = "000q362u0o7m16040c80020e1g2q0u061i2m100g0s12461k1e0a484a2o0k0i4m3m2k3o2c084g3u3q4i403s424kb0au4q9i4c5oas52349mb25q0m3g184438bab4b65g5i3cbc5k4s3a144u5m604ob8bubs5s9a51a65ube9obh9c1c559e62bi9gc04fc2c4c630c86eca56a8585b6g5c64cc66bkce1m5e6k6s3i1u686abm6j6v6c3eaadq326mae2s6o70dobobq6qacch7c76782eci72cm7k74cqckds1a9kcs2gd8cudv2je07ee228gu7ge4d47ada20d67id0e8e6267oeaco7s3k1sh0eu7q7uemd282eo1q86f0ecdceqeeajeg85f2de22ei88etagf4dgf6didkfa8aek8ch2f88gdmfcfe8efg968ififkfo9q8kfmg01ofs8mis248ofq8u8q8sg29takanaogkgah498g49092fu95gcg6geg8gmgggo2agikekggqgskjaqkpl1l5h6h8hahckklskmhehqhukq9ul2hghia2hkl7a0i9kskul8lai6hti0iai2lclqa4lei4imlphmj8lum0igm6lgm8m2m4mpikmamsmuieiimqmcmen0mgmin6n2n8nalkhon4ncmkneioningnmliomokiqnoo0j0o4o2ooj4j2j6k6mmo6nqjaornsiuosoujgjeicp8p0pap4p6p2pqnkpsjdpupmpcq0o8ogq2jipijkjqoaocnupopkoepeq6jooiq8jmpgqaq4jsqcqeqgqkr0juqiqoqmk0qsquk2k8k4r6r8qqkakcr2rar4rcrerqrslmrgrirkrmros1sdrus2seshs5s6s8sasqsjsksmsosuss"


def _low(engs, n, skip=0):
    m = 0
    for e in engs[skip:skip + n]:
        m |= 1 << e
    return m


def _roles(T, topo):
    cores = list(T.cores)
    chips = sorted(set(topo.chip(c) for c in cores))
    side = [[q for q, c in enumerate(cores) if topo.chip(c) == ch] for ch in chips]
    partner, helper = {}, {}
    for s in range(2):
        first = cores[side[s][0]]
        spare = [c for c in topo.cores_of(first) if c not in cores and topo.die(c) != topo.die(first)]
        for i, q in enumerate(side[s]):
            partner[q] = side[1 - s][i]
            helper[q] = spare[i]
    return cores, side, partner, helper


def _ap(T, name, lo=0, hi=None):
    pool, a, n = LAY[name]
    return T["pool" + pool][:, a + lo:a + (n if hi is None else hi)]


def _via_cols(q, side):
    return (side[0][0] if q in side[0] else side[1][0]) * 384


def _helper_program(g, core, q, T, topo):
    cores, side, partner, helper = _roles(T, topo)
    dst = cores[partner[q]]
    rid, pid, _ = topo.addr(dst)
    nin, nout = len(topo.engines(cores[q], core)), len(topo.engines(core, dst))
    w = L // 2 // NCH
    c0 = _via_cols(q, side)
    for rho in range(RO):
        for k in range(NCH):
            g.wait_ge(T.sem["h%d" % (rho * NCH + k)], nin)
            piece = _ap(T, "XP%d" % rho, c0 + k * w, c0 + (k + 1) * w)
            g.remote_dma(piece, piece, T.sem["xp%d" % rho], T.sem.sent, pid, rid, topo.mask(core, dst))
    g.wait_ge(T.sem.sent, RO * NCH * nout)


def rank_program(g, core, T, topo):
    cores, side, partner, helper = _roles(T, topo)
    q = T.rank_of(core)
    if q is None:
        for r, h in helper.items():
            if h == core:
                _helper_program(g, core, r, T, topo)
        return
    mine = side[0] if q in side[0] else side[1]
    other = side[1] if q in side[0] else side[0]
    ops = []
    V, S = g.vector, g.scalar

    def R(name, lo=0, hi=None, step=1, rows=None):
        pool, a, n = LAY[name]
        hi = n if hi is None else hi
        t = T["pool" + pool]
        rows = slice(0, 128) if rows is None else rows
        ap = t[rows, a + lo:a + hi] if step == 1 else t[rows, a + lo:a + hi:step]
        return (ap, pool, a + lo, a + hi, (hi - lo + step - 1) // step)

    def P(bank, lo, hi, step=1):
        t = T["ps%d" % bank]
        return (t[:, lo:hi] if step == 1 else t[:, lo:hi:step], "ps%d" % bank, lo, hi, (hi - lo + step - 1) // step)

    def RT(lo, hi, w=24):
        ap = T.roots[:, lo, 0:w] if hi == lo + 1 else T.roots[:, lo:hi, 0:w]
        return (ap, "roots", lo, hi, (hi - lo) * w)

    def add(alts, reads, writes, lat=0.0, kind="c", deps=(), sem=None, cnt=0):
        ops.append([alts, list(reads), list(writes), lat, kind, list(deps), sem, cnt])
        return len(ops) - 1

    def cyc(out, in_):
        return out[4] * (0.5 if out[1] in "bhu" and in_[1] in "bhu" else 1)

    def val(s):
        return s[0] if isinstance(s, tuple) else s

    def ts(out, in0, s1, s2, op0, op1=None, alt=None):
        rd = [in0] + [s for s in (s1, s2) if isinstance(s, tuple)]
        if op1 is None:
            alts = {"v": (lambda: V.tensor_scalar(out[0], in0[0], val(s1), None, op0), "cyc", cyc(out, in0))}
        else:
            alts = {"v": (lambda: V.tensor_scalar(out[0], in0[0], val(s1), val(s2), op0, op1), "cyc", cyc(out, in0))}
        if alt is not None:
            func, bias, scale = alt
            alts["a"] = (lambda: S.activation(out[0], in0[0], func, bias=val(bias), scale=scale), "cyc", out[4])
        return add(alts, rd, [out])

    def aff(out, in_, scale, bias=0.0):
        return ts(out, in_, scale, bias, OP.mult, OP.add, alt=(AF.Identity, bias, scale))

    def tt(out, in0, in1, op):
        n = out[4] * (1 if in0[1][:2] == "ps" or in1[1][:2] == "ps" else 2)
        return add({"v": (lambda: V.tensor_tensor(out[0], in0[0], in1[0], op), "cyc", n)}, [in0, in1], [out])

    def cp(out, in_, flex=False):
        alts = {"v": (lambda: V.tensor_copy(out[0], in_[0]), "cyc", cyc(out, in_))}
        if flex:
            alts["a"] = (lambda: S.activation(out[0], in_[0], AF.Copy), "cyc", out[4])
        return add(alts, [in_], [out])

    def ms(out, c):
        return add({"v": (lambda: V.memset(out[0], c), "cyc", cyc(out, out))}, [], [out])

    def gather(out, win, off, in1=None, op=None, flex=True):
        if in1 is not None:
            return add({"v": (lambda: V.tensor_tensor(out[0], win[0].indirect(off[0]), in1[0], op), "ga", out[4])}, [win, off, in1], [out])
        alts = {"v": (lambda: V.tensor_copy(out[0], win[0].indirect(off[0])), "ga", out[4])}
        if flex:
            alts["a"] = (lambda: S.activation(out[0], win[0].indirect(off[0]), AF.Copy), "ga", out[4])
        return add(alts, [win, off], [out])

    def scatter(qu, win, off, in_, plus=None):
        if qu == "a":
            call = lambda: S.activation(win[0].indirect(off[0]), in_[0], AF.Silu)
        elif plus is None:
            call = lambda: V.tensor_copy(win[0].indirect(off[0]), in_[0])
        else:
            call = lambda: V.tensor_scalar(win[0].indirect(off[0]), in_[0], 1.0, plus, OP.mult, OP.add)
        return add({qu: (call, "sc", in_[4])}, [in_, off], [win])

    def scan(out, in_, first):
        on = R("ONES", 0, out[4])
        rd = [on, in_] + ([first] if isinstance(first, tuple) else [])
        return add({"v": (lambda: V.tensor_tensor_scan(out[0], on[0], in_[0], val(first), OP.mult, OP.add), "cyc", out[4])}, rd, [out])

    def mms(items):
        def call():
            return [g.tensor.matmul(o[0], a[0], b[0], s, e) for o, a, b, s, e in items]
        rd, wr = [], []
        for o, a, b, s, e in items:
            rd += [a, b]
            wr.append(o)
        return add({"t": (call, "pe", sum(max(64, it[2][4]) for it in items))}, rd, wr, cnt=len(items))

    def F(x, y):
        return R("F", x * 144 + 16 - y, x * 144 + 144 - y)

    def wrap(out, row, n, src, start=True, stop=True):
        mat = (lambda r: F(src, r)) if isinstance(src, int) else (lambda r: R(src, 16 - r, 144 - r))
        return [(out, mat(r), R(row, r, n, 16), start and r == 0, stop and r == 15) for r in range(16)]

    nd = [0]

    def dma(qu, out, in_, kb):
        sem = T.sem["d%d" % nd[0]]
        nd[0] += 1
        eng = g.sync if qu == "s" else S
        return add({qu: (lambda: eng.dma_start(out[0], in_[0]), "us", 0.06)}, [in_], [out], 1.9 + kb / 250.0, "d", (), sem, 16)

    def hbm(ap, name):
        return (ap, name, 0, 1, 1)

    def iota(out, pat, base, cm):
        if out[1] == "i":
            call = lambda: g.iota(out[0], pat, base, cm)
        else:
            call = lambda: g.iota(out[0], pat, base, cm, allow_small_or_imprecise_dtypes=True)
        return add({"g": (call, "cyc", 130 + 2 * out[4])}, [], [out])

    def sel(out, in_, pat, op, base, cm):
        return add({"g": (lambda: g.affine_select(out[0], in_[0], pat, op, 0.0, base, cm), "cyc", 170 + 2 * out[4])}, [in_], [out])

    sent = [0]
    last_remote = [None]

    def remote(items, deps=()):
        def call():
            if len(items) == 1:
                c, d, s, sem, m = items[0]
                rid, pid, _ = topo.addr(c)
                g.remote_dma(d, s[0], sem, T.sem.sent, pid, rid, m)
            else:
                tr = []
                for c, d, s, sem, m in items:
                    rid, pid, _ = topo.addr(c)
                    tr.append(RemoteDMATransfer(dst_ids=[DstId(rid=rid, pnc=pid)], dma_engine_mask=m, remote_sem=sem, src=s[0], dst=d))
                g.remote_dma_fused(tr, local_sem=T.sem.sent)
        sent[0] += sum(bin(it[4]).count("1") for it in items)
        dp = list(deps) + ([last_remote[0]] if last_remote[0] is not None else [])
        last_remote[0] = add({"g": (call, "us", 0.5)}, [it[2] for it in items], [], 0.0, "r", dp)
        return last_remote[0]

    def arrival(writes, sem, cnt, after, lat):
        return add({"x": (None, "us", 0.0)}, [], writes, lat, "x" if cnt else "n", after, sem, cnt)

    via = _via_cols(q, side)
    dirc = L // 2 - via
    rows0, rows1, rows15, one = slice(0, 128, 16), slice(1, 128, 16), slice(15, 128, 16), slice(0, 1)
    dma("s", R("K", 0, 192), hbm(T.kids[:, 0:192], "kids"), 100)
    dma("a", R("H0", via, via + 1536), hbm(T.x[:, via:via + 1536], "x"), 500)
    dma("s", R("H0", dirc, dirc + 1536), hbm(T.x[:, dirc:dirc + 1536], "x"), 500)
    ms(R("ZT"), 0.0)
    dma("s", R("WA", rows=rows0), R("ZT"), 130)
    dma("a", R("WD", rows=rows0), R("ZT"), 130)
    dma("s", R("ML"), hbm(T.ml[:], "ml"), 30)
    dma("a", R("MR"), hbm(T.mr[:], "mr"), 30)
    dma("s", R("W"), hbm(T.w[:], "w"), 30)
    dma("s", R("K", 192, 384), hbm(T.kids[:, 192:384], "kids"), 100)
    for k in range(2):
        iota(R("IO0", 512 * k, 512 * k + 512), [[1, 32], [64, 16]], int(EPOCH[0]) + 32 * k, 0)
    ms(R("ONES"), 1.0)
    ms(R("CR"), -0.375)
    ms(R("Y1"), 0.0)
    ms(R("F"), 0.0)
    sel(R("T9"), R("ONES", 0, 9), [[-16, 9]], OP.is_ge, 16, 1)
    sel(R("Y1", 0, 144, 16), R("T9"), [[16, 9]], OP.is_ge, -1, -1)
    sel(R("F", 0, 2304, 16), R("ONES", 0, 144), [[-1, 16], [-16, 9]], OP.is_equal, 16, 1)
    sel(R("BH"), R("ONES", 0, 128), [[-16, 8], [0, 16]], OP.is_ge, 0, 1)
    sel(R("BON"), R("BH"), [[16, 8], [0, 16]], OP.is_ge, 15, -1)
    sel(R("TRI"), R("BON"), [[1, 128]], OP.is_ge, 0, -1)
    sel(R("TRS"), R("BON"), [[1, 128]], OP.is_gt, 0, -1)
    sel(R("EYE"), R("ONES", 0, 128), [[-1, 128]], OP.is_equal, 0, 1)
    iota(R("PI"), [[1, 1]], 0, 1)
    iota(R("PLa"), [[1, 8], [128, 8]], 0, 0)
    for k in range(4):
        iota(R("IOP", 256 * k, 256 * k + 256), [[1, 2], [128, 8], [8, 16]], 2 * k, 0)
        iota(R("IO1", 256 * k, 256 * k + 256), [[1, 16], [64, 16]], int(EPOCH[1]) + 16 * k, 0)
        iota(R("IO1", 1024 + 256 * k, 1280 + 256 * k), [[1, 16], [64, 16]], int(EPOCH[1]) + 1024 + 16 * k, 0)
    ts(R("PM"), R("PI"), 15, None, OP.bitwise_and)
    ts(R("PM8"), R("PM"), 8.0, None, OP.mult)
    ts(R("BIGC"), R("PM"), 12.0, 10000.0, OP.is_ge, OP.mult)
    aff(R("PL"), R("PLa"), 1.0, R("PM8"))
    ts(R("WS"), R("Y1"), R("W"), None, OP.mult)
    aff(R("ML4"), R("ML"), 0.25)
    aff(R("MR4"), R("MR"), 0.25)
    for r in (R("TR", 1024, 1032), R("TB2", 1024, 1032), R("TS", 0, 8), R("FXA"), R("FXD"), RT(0, 8), RT(8, 16)):
        ms(r, 0.0)
    for win in ("VA", "VD"):
        for rows in (rows0, rows1):
            dma("s", R(win, rows=rows), R("ZT", 0, 194), 100)

    on_chip = topo.engines(core, helper[q])
    full = topo.mask(core, helper[q])
    half = len(on_chip) // 2
    lo_half, hi_half = _low(on_chip, half), _low(on_chip, half, half)
    pcore = cores[partner[q]]
    far_mask = topo.mask(core, pcore)
    nfar = len(topo.engines(core, pcore))

    def ship_via(rho):
        w = L // 2 // NCH
        last = None
        for k in range(NCH):
            a = via + k * w
            last = remote([(helper[q], _ap(T, "XP%d" % rho, a, a + w), R("H%d" % rho, a, a + w), T.sem["h%d" % (rho * NCH + k)], full)])
        return arrival([], None, 0, [last], 8.0)

    def ship_direct(rho, first, deps=()):
        last = remote([(pcore, _ap(T, "XP%d" % rho, dirc, dirc + 1536), R("H%d" % rho, dirc, dirc + 1536), T.sem["xp%d" % rho], far_mask)], deps)
        arrival([R("XP%d" % rho)], T.sem["xp%d" % rho], (NCH + 1) * nfar, [first, last], 14.0)

    def sizes(rho):
        s = str(rho)

        def r(name, lo=0, hi=None, step=1):
            return R(name + s, lo, hi, step)
        for lo, hi in (((64, 192), (0, 64)) if rho == 0 else ((0, 192),)):
            K = R("K", 192 * rho + lo, 192 * rho + hi)
            ts(r("kc", lo, hi), K, 4, None, OP.arith_shift_right)
            ts(r("t1", lo, hi), r("kc", lo, hi), -4095.0 / 256.0, None, OP.mult)
            tt(r("t2", lo, hi), r("t1", lo, hi), K, OP.add)
            ts(r("SU", lo, hi), r("t2", lo, hi), 256.0, None, OP.mult)
        K = R("K", 192 * rho, 192 * rho + 192)
        cp(r("Kf"), K)
        cp(r("KU"), K)
        ts(r("SZ", 64, 192), r("Kf", 64, 192), 3072.0, 1.0, OP.is_ge, OP.add)
        o, i = r("red"), r("SZ", 64, 192)
        add({"v": (lambda: V.tensor_reduce(o[0], i[0], AX.X, OP.add), "cyc", 128)}, [i], [o])
        aff(r("rb"), r("red"), 1.0, -128.0)
        aff(r("n1"), r("SZ", 64, 192), -16384.0, 16384.0 - OFFS)
        tt(r("n2"), r("n1"), r("Kf", 64, 192), OP.add)
        ts(r("IDS", 64, 192), r("n2"), -8192.0, None, OP.max)
        aff(r("IDS", 0, 64), r("Kf", 0, 64), 1.0, -OFFS)
        tt(r("SUM"), r("IDS", 0, 160), r("IDS", 32, 192), OP.add)
        tt(r("sz1"), r("SZ", 64, 96), r("SZ", 96, 128), OP.add)
        aff(r("s1b"), r("sz1"), 1.0, -2.0)
        mms([(P(7, k, 512, 16), F(k, 0), r("s1b"), True, True) for k in range(16)])
        cp(R("TS", 8, 520), P(7, 0, 512), True)
        ts(r("LS"), r("Kf", 128, 192), -3576.0, 0.0, OP.add, OP.max)
        for k in range(2):
            gather(R("GS", 512 * k, 512 * k + 512), R("TS"), r("LS", 32 * k, 32 * k + 32))
        mms(wrap(P(7, 0, 64), "GS", 1024, 0) + [(P(7, 64, 65), R("BON"), r("rb"), True, True)])
        aff(r("EN", 0, 1), P(7, 64, 65), 1.0, -OFFS)
        tt(r("SZ", 128, 192), P(7, 0, 64), r("SZ", 128, 192), OP.add)
        tt(r("RSb", 256, 288), r("SZ", 128, 160), r("SZ", 160, 192), OP.add)

    def marks(rho, chunks, names):
        s = str(rho)
        io = "IO" + s
        for i in chunks:
            off = R("SU" + s, 16 * i, 16 * i + 16)
            a = 256 * (i - 4 if i >= 4 else i)
            if MARKS[rho][i] == "a":
                scatter("a", R("WA"), off, R(io, a, a + 256))
            else:
                scatter("v", R("WD"), off, R(io, a % 1024, a % 1024 + 256), float(a - a % 1024))
        return [dma("s", R(name + s), R(win, rows=rows0), 130) for name, win in names]

    def both(out, tiles, lo, hi):
        if len(tiles) == 1:
            return R(tiles[0], lo, hi)
        tt(R(out, lo, hi), R(tiles[0], lo, hi), R(tiles[1], lo, hi), OP.max)
        return R(out, lo, hi)

    def structure(rho):
        s = str(rho)
        E = EPOCH[rho]

        def r(name, lo=0, hi=None, step=1):
            return R(name + s, lo, hi, step)
        who = MARKS[rho]
        n1 = [x for x, k in ((("IA", "WA"), "a"), (("ID", "WD"), "v")) if k in who[4:]]
        n2 = [x for x, k in ((("JA", "WA"), "a"), (("JD", "WD"), "v")) if k in who[:4]]
        marks(rho, range(4, 12), n1)
        done = marks(rho, range(4), n2)
        last = {w: n for n, w in n1 + n2}
        comb = both("comb" + s, [n + s for n, w in n1], 192, 256)
        ts(r("miss"), comb, E - 0.5, None, OP.is_lt)
        aff(r("RSb", 192, 224), r("miss", 0, 32), 2.0)
        tt(r("RSb", 224, 256), r("miss", 32, 64), r("sz1"), OP.mult)
        mms([(P(5, 0, 96), R("BON"), r("RSb", 192, 288), True, True), (P(5, 96, 192), R("TRS"), r("RSb", 192, 288), True, True)])
        scan(r("EN", 1, 97), P(5, 0, 96), r("EN", 0, 1))
        tt(r("RS"), P(5, 96, 192), r("EN", 0, 96), OP.add)
        ts(r("sv"), comb, MAGIC - E, MAGIC, OP.add, OP.subtract)
        aff(r("big"), r("miss"), 8192.0)
        tt(r("svb"), r("sv"), r("big"), OP.add)
        ts(r("L1"), r("svb", 0, 32), 1024.0, None, OP.min)
        ts(r("I2", 0, 64), r("svb"), -1024.0, 1024.0, OP.add, OP.min)
        ts(r("I2", 64, 96), r("svb", 32, 64), -1024.0, 1024.0, OP.add, OP.min)
        ts(r("L2", 32, 64), r("svb", 32, 64), -1024.0, 1024.0, OP.add, OP.min)
        tt(r("PRE", 0, 32), r("miss", 0, 32), r("RS", 0, 32), OP.mult)
        tt(r("ADD"), r("miss", 32, 64), r("RS", 32, 64), OP.mult)
        comb = both("comb" + s, [n + s for n in last.values()], 0, 192)
        ts(r("RSb", 0, 192), comb, E - 0.5, None, OP.is_lt)
        mms([(P(6, 0, 192), R("BON"), r("RSb", 0, 192), True, True), (P(6, 192, 384), R("TRI"), r("RSb", 0, 192), True, True)])
        ms(r("EX", 0, 1), 0.0)
        ms(r("T", 192, 200), 0.0)
        scan(r("EX", 1, 193), P(6, 0, 192), 0.0)
        tt(r("T", 0, 192), P(6, 192, 384), r("EX", 0, 192), OP.add)
        cp(r("inh"), r("EX", 1, 193))
        mms([(P(6, 384, 400), F(0, p), r("inh", p, 192, 12), p == 0, p == 11) for p in range(12)]
            + [(P(6, 400, 401), F(0, p), r("inh", 12 * p + 11, 12 * p + 12), p == 0, p == 15) for p in range(16)])
        ms(r("TB", 16, 24), 10000.0)
        aff(r("nb"), P(6, 400, 401), -1.0, 0.5)
        aff(r("TB", 0, 16), P(6, 384, 400), 1.0, R("BIGC"))
        for k in range(2):
            o, i, b = R("CA", 512 * k, 512 * k + 512), R("IOP", 512 * k, 512 * k + 512), r("nb")
            add({"a": (lambda o=o, i=i, b=b: S.activation(o[0], i[0], AF.Sign, bias=b[0]), "cyc", 512)}, [i, b], [o])
        mms(wrap(P(6, 0, 64), "CA", 1024, "Y1"))
        ts(r("a16"), P(6, 0, 64), 0.5, 8.0, OP.mult, OP.add)
        aff(r("af"), P(6, 0, 64), 6.0, 96.0)
        for k in range(2):
            gather(R("CB", 512 * k, 512 * k + 512), r("TB"), r("a16", 32 * k, 32 * k + 32), R("IOP", 512 * k, 512 * k + 512), OP.is_le)
        mms(wrap(P(6, 64, 128), "CB", 1024, "Y1"))
        tt(r("colf"), P(6, 64, 128), r("af"), OP.add)
        cp(r("c16"), r("colf"))
        for k in range(2):
            gather(R("CC", 512 * k, 512 * k + 512), r("T"), r("c16", 32 * k, 32 * k + 32), R("IOP", 512 * k, 512 * k + 512), OP.is_le)
        ts(r("inv"), R("PL"), r("EX", 192, 193), -32768.0, OP.is_ge, OP.mult)
        aff(r("bs"), r("colf"), 16.0)
        o = P(6, 128, 192)
        mms([(o, R("EYE"), r("inv"), True, False), (o, R("EYE"), r("bs"), False, False)] + wrap(o, "CC", 1024, "Y1", False))
        aff(RT(8 * rho, 8 * rho + 8, 8), o, 1.0, E)
        return done

    def table(name, items):
        for b in range(2):
            mms([it for k in range(8) for it in items(3 + b, 64 * k, 8 * b + k)])
            cp(R(name, 512 * b, 512 * b + 512), P(3 + b, 0, 512), True)

    def trees(rho):
        s = str(rho)
        E = EPOCH[rho]
        H = "H" + s

        def r(name, lo=0, hi=None, step=1):
            return R(name + s, lo, hi, step)

        def to_pos(m, lo, hi):
            ts(r("y", lo, hi), m, -63.5, MAG128, OP.add, OP.add)
            ts(r("p1", lo, hi), r("y", lo, hi), MAG128, -3071.0 / 3072.0, OP.subtract, OP.mult)
            tt(r("p2", lo, hi), m, r("p1", lo, hi), OP.add)
            ts(r("OFF", lo, hi), r("p2", lo, hi), 24.0, 12.25, OP.mult, OP.add)

        mo = P(0, 64, 128)
        for t in range(3):
            ha = "HA%d" % t
            win = R(H, 0, L + NB * t)
            gather(R(ha, 0, 512), win, r("KU", 64 * t, 64 * t + 32))
            gather(R(ha, 512, 1024), win, r("KU", 64 * t + 32, 64 * t + 64))
            if t < 2:
                mms([(P(0, 0, 512), R("CR", rows=one), R("ONES", rows=one), True, False)])
                mms([(P(0, 0, 512), R("ML4"), R(ha, 0, 512), False, False)])
                mms([(P(0, 0, 512), R("MR4"), R(ha, 512, 1024), False, True)])
                ts(R("NT"), P(0, 0, 512), MAGIC, MAGIC, OP.add, OP.subtract)
                ts(R(H, L + NB * t, L + NB * t + NB), R("NT"), -127.0, 127.0, OP.max, OP.min)
            a, b, c = 64 * t, 64 * t + 32, 64 * t + 64
            n0, n1 = 32 * t, 32 * t + 32
            mms(wrap(P(1, a, c), ha, 1024, "WS"))
            cp(r("cp", n0, n1), P(1, b, c), True)
            tt(r("SW", b, c), P(1, a, b), r("cp", n0, n1), OP.is_lt)
            if t < 2:
                aff(r("SW", a, b), r("SW", b, c), -1.0, 1.0)
            else:
                tt(r("SW", a, b), P(1, a, b), r("cp", n0, n1), OP.is_ge)
            if t > 0:
                tt(r("P", a, c), r("SW", a, c), r("SZ", a, c), OP.mult)
                x, base = ("X1", r("ADD")) if t == 1 else ("X2", r("RS", 64, 96))
                tt(r(x, 0, 32), r("P", b, c), base, OP.add)
                tt(r(x, 32, 64), r("P", a, b), base, OP.add)
                tt(r("szf", n0, n1), r("P", a, b), r("P", b, c), OP.add)
            tt(r("Q", a, c), r("SW", a, c), r("IDS", a, c), OP.mult)
            tt(r("A", n0, n1), r("Q", a, b), r("Q", b, c), OP.add)
            tt(r("B", n0, n1), r("SUM", a, b), r("A", n0, n1), OP.subtract)
            mms([(P(2, k, 512, 16), F(k, j), r("AB"[j], n0, n1), j == 0, j == 1) for k in range(16) for j in range(2)])
            ts(R("V%d" % t), P(2, 0, 512), OFFS + E, 0.0, OP.add, OP.max, alt=(AF.Relu, OFFS + E, 1.0))
            if t == 1:
                table("TR", lambda bk, c0, k: [(P(bk, c0, c0 + 64), F(k, 1), r("X1"), True, False),
                                               (P(bk, c0, c0 + 64), F(k, 0), r("I2", 32, 96), False, True)])
                gather(R("G1"), R("TR"), r("L1"), flex=False)
                mms(wrap(P(0, 0, 32), "G1", 512, 0))
                tt(r("i0"), P(0, 0, 32), r("I2", 0, 32), OP.max)
                cp(r("L2", 0, 32), r("i0"))
                tt(r("PRE", 32, 64), r("szf", 32, 64), r("ADD"), OP.add)
                mms([(mo, R("EYE"), r("PRE"), True, False), (P(0, 64, 96), R("ONES", 0, 128, rows=one), R("ONES", 0, 32, rows=one), False, False)]
                    + wrap(P(0, 64, 96), "G1", 512, 1, False, False))
        table("TB2", lambda bk, c0, k: [(P(bk, c0, c0 + 64), F(k, 0), r("X2"), True, True)])
        tt(r("m"), r("RS", 64, 96), r("szf", 64, 96), OP.add)
        to_pos(r("m"), 64, 96)
        scatter("a", R("VA"), r("OFF", 64, 96), R("V2"))
        gather(R("G2"), R("TB2"), r("L2"), flex=False)
        mms(wrap(mo, "G2", 1024, 0, False))
        to_pos(mo, 0, 64)
        scatter("v", R("VD"), r("OFF", 0, 32), R("V0"))
        scatter("a", R("VA"), r("OFF", 32, 64), R("V1"))
        for qu, win, k in (("s", "VD", "D"), ("a", "VA", "A")):
            dma(qu, R("T%sa" % k), R(win, 24, 3096, rows=rows0), 100)
            dma(qu, R("T%sb" % k), R(win, 0, 3072, rows=rows1), 100)
            dma(qu, R("FX" + k, 0, 23, rows=rows15), R(win, 1, 24, rows=rows0), 1)
        for k in "DA":
            tt(RT(8 * rho + 7, 8 * rho + 8), RT(8 * rho + 7, 8 * rho + 8), R("FX" + k), OP.max)
        for b, d in enumerate((other[0], mine[0])):
            c0 = 24 * d
            u = P(7, 96 * b, 96 * b + 96)
            tt(u, R("TDa", c0, c0 + 96), R("TDb", c0, c0 + 96), OP.max)
            for x in (R("TAa", c0, c0 + 96), R("TAb", c0, c0 + 96), RT(8 * rho + d, 8 * rho + d + 4)):
                tt(u, u, x, OP.max)
            ts(r("AT", c0, c0 + 96), u, MAGIC - E, MAGIC, OP.add, OP.subtract)

    def exchange(rho):
        s = str(rho)
        nxt = "H%d" % (rho + 1)
        c0 = other[0] * 24
        sl = remote([(pcore, _ap(T, "LP" + s), R("AT" + s, c0, c0 + 96), T.sem["lp" + s], far_mask)])
        arrival([R("LP" + s)], T.sem["lp" + s], nfar, [sl], 2.2)
        rest = [mine[(mine.index(q) + k) % len(mine)] for k in range(1, len(mine))]
        for b, (src, win, lst, l0, sem) in enumerate(((q, R("H" + s, 0, L), "AT" + s, mine[0] * 24, "own" + s),
                                                      (partner[q], R("XP" + s), "LP" + s, 0, "far" + s))):
            def off(r):
                a = l0 + 24 * mine.index(r)
                return R(lst, a, a + 24)
            stg = [R("STG" + s, 384 * (3 * b + k), 384 * (3 * b + k) + 384) for k in range(3)]
            land = _ap(T, nxt, 384 * src, 384 * src + 384)
            for k in range(3):
                gather(stg[k], win, off(rest[k]))
            gather(R(nxt, 384 * src, 384 * src + 384), win, off(q))
            remote([(cores[rest[0]], land, stg[0], T.sem[sem], lo_half), (cores[rest[1]], land, stg[1], T.sem[sem], hi_half)])
            last = remote([(cores[rest[2]], land, stg[2], T.sem[sem], full)])
            froms = [r if b == 0 else partner[r] for r in rest]
            arrival([R(nxt, 384 * r, 384 * r + 384) for r in froms], T.sem[sem], 2 * len(on_chip), [last], 2.6)

    first = ship_via(0)
    sizes(0)
    ship_direct(0, first, structure(0))
    sizes(1)
    trees(0)
    structure(1)
    exchange(0)
    first = ship_via(1)
    ship_direct(1, first)
    trees(1)
    exchange(1)
    for qu, a, w in (("s", via, 1536), ("a", dirc, 768), ("s", dirc + 768, 768)):
        dma(qu, hbm(T.y[:, a:a + w], "y%d" % a), R("H2", a, a + w), w // 4)

    _emit(g, T, ops, sent[0])


def _deps(ops):
    deps = [{j: True for j in o[5]} for o in ops]
    seen = {}
    for i, o in enumerate(ops):
        acc = set((r[1], r[2], r[3], False) for r in o[1]) | set((r[1], r[2], r[3], True) for r in o[2])
        for sp, lo, hi, wr in sorted(acc):
            for j, lo2, hi2, wr2 in seen.get(sp, ()):
                if lo < hi2 and lo2 < hi and (wr or wr2):
                    deps[i][j] = True
                elif sp[:2] == "ps" and not (list(ops[j][0]) == list(o[0]) == ["v"]):
                    deps[i].setdefault(j, False)
        for sp, lo, hi, wr in sorted(acc):
            seen.setdefault(sp, []).append((i, lo, hi, wr))
    return deps


def _order(ops, deps):
    code = [DIGITS.index(ORDER[p]) * 32 + DIGITS.index(ORDER[p + 1]) for p in range(0, len(ORDER), 2)]
    queue = [sorted(o[0])[0] for o in ops]
    for c in code:
        if c % 2:
            queue[c // 2] = "v"
    done, order = [False] * len(ops), []
    for i in [c // 2 for c in code] + list(range(len(ops))):
        stack = [i]
        while stack:
            a = stack[-1]
            wait = [] if done[a] else [j for j in sorted(deps[a]) if not done[j]]
            if wait:
                stack.extend(wait[::-1])
                continue
            if not done[a]:
                done[a] = True
                order.append(a)
            stack.pop()
    return order, queue


def _emit(g, T, ops, nsent):
    deps = _deps(ops)
    order, queue = _order(ops, deps)
    counter = {"v": T.sem.cv, "a": T.sem.ca, "t": T.sem.ct, "g": T.sem.cg}
    total = {k: 0 for k in counter}
    token = {}
    for i in order:
        o, k = ops[i], queue[i]
        if o[4] == "c":
            total[k] += o[7] or 1
            token[i] = ("c" + k, counter[k], total[k])
        elif o[4] in "dx":
            token[i] = (i, o[6], o[7])
    eng = {"v": g.vector, "a": g.scalar, "t": g.tensor, "g": g, "s": g.sync}
    waited = {k: {} for k in eng}
    for i in order:
        o, k = ops[i], queue[i]
        if k == "x":
            continue
        need = {}
        for j in sorted(deps[i]):
            if j in token and not (queue[j] == k and (k == "t" or not deps[i][j])):
                key, sem, v = token[j]
                if v > waited[k].get(key, 0) and v > need.get(key, (None, 0))[1]:
                    need[key] = (sem, v)
        for key, (sem, v) in need.items():
            eng[k].wait_ge(sem, v)
            waited[k][key] = v
        res = o[0][k][0]()
        if o[4] == "d":
            res.then_inc(o[6], 16)
        elif k == "t":
            for ins in res:
                ins.then_inc(counter["t"], 1)
        elif o[4] == "c":
            res.then_inc(counter[k], 1)
    for k in counter:
        g.wait_ge(counter[k], total[k])
    for i in order:
        if ops[i][4] in "dx" and not any(i in w for w in waited.values()):
            g.wait_ge(ops[i][6], ops[i][7])
    g.wait_ge(T.sem.sent, nsent)
